import numpy as np, ml_dtypes
CORES = [7,15,23,39,47,63,71,79,87,95,119,127]
N = 12
GR, GC = 4, 3
L, KA, KB, F = 12, 4, 3, 512
def setup_inputs(rng):
    return {"a": rng.standard_normal((N, 128, KA * 128), dtype=np.float32).astype(ml_dtypes.bfloat16), "b": rng.standard_normal((N, 128, KB * F), dtype=np.float32).astype(ml_dtypes.bfloat16)}
def reference(a, b):
    A, B = a.astype(np.float64), b.astype(np.float64)
    y = np.zeros((N, 128, F))
    for i in range(GR):
        for j in range(GC):
            for k in range(L):
                At = A[i * GC + k // KA][:, 128 * (k % KA):128 * (k % KA) + 128]
                Bt = B[(k // KB) * GC + j][:, F * (k % KB):F * (k % KB) + F]
                y[i * GC + j] += At.T @ Bt
    return {"y": y.astype(ml_dtypes.bfloat16 if a.dtype != np.float64 else np.float64)}

from concourse.bass import DstId, RemoteDMATransfer
from concourse.mybir import AluOpType

GR, GC = 4, 3
L, KA, KB, F = 12, 4, 3, 512
M = 128
NENG = 8

SCRATCH = {
    "abuf": ("sbuf", [128, KA * M], "bfloat16"),
    "bbuf": ("sbuf", [128, KB * F], "bfloat16"),
    "arecv": ("sbuf", [128, GR * KB * M], "bfloat16"),
    "pbuf": ("sbuf", [128, 3 * F], "bfloat16"),
    "precv": ("sbuf", [128, 3 * F], "bfloat16"),
    "ybuf": ("sbuf", [128, F], "bfloat16"),
    "ps0": ("psum", [128, F], "float32"),
    "ps1": ("psum", [128, F], "float32"),
    "ps2": ("psum", [128, F], "float32"),
    "ps3": ("psum", [128, F], "float32"),
    "acc0": ("psum", [128, F], "float32"),
    "acc1": ("psum", [128, F], "float32"),
}
SEMAPHORES = (["a_in", "b_in", "sent", "y_done", "stored"]
              + ["A%d" % i for i in range(GR)] + ["mm%d" % n for n in range(4)]
              + ["cp%d" % n for n in range(3)] + ["P%d" % n for n in range(3)] + ["ad%d" % n for n in range(2)])


def pick(mask, n):
    bits = [e for e in range(mask.bit_length()) if (mask >> e) & 1][:n]
    return sum(1 << e for e in bits)


def rank_program(g, core, T, topo):
    rank = T.rank_of(core)
    if rank is None:
        return
    r, j = divmod(rank, GC)
    cores = T.cores
    sem = T.sem

    def holder(i, k):
        return i * GC + k // KA

    def send_order(row):
        return [(row + 1) % GR, (row + 3) % GR, (row + 2) % GR]

    g.sync.dma_start(T.abuf[:], T.a[:]).then_inc(sem.a_in, 16)
    g.sync.dma_start(T.bbuf[:], T.b[:]).then_inc(sem.b_in, 16)

    sent = 0
    g.wait_ge(sem.a_in, 16)
    my_ks = list(range(KA * j, KA * j + KA))
    rows = sorted(set(k // KB for k in my_ks), key=lambda q: ((q - r) % 2 == 0, q))
    for q in rows:
        ks = [k for k in my_ks if k // KB == q]
        dsts = [q * GC + c for c in range(GC) if q * GC + c != rank]
        mask = topo.mask(core, cores[dsts[0]])
        for d in dsts:
            assert topo.may_write(core, cores[d])
            mask &= topo.mask(core, cores[d])
        mask = pick(mask, NENG)
        lo = (r * KB + ks[0] - KB * q) * M
        tr = RemoteDMATransfer(
            dst_ids=[DstId(rid=topo.addr(cores[d])[0], pnc=topo.addr(cores[d])[1]) for d in dsts],
            dma_engine_mask=mask, remote_sem=sem["A%d" % r],
            srcs=[T.abuf[:, (ks[0] % KA) * M:(ks[-1] % KA + 1) * M]],
            dsts=[T.arecv[:, lo:lo + len(ks) * M] for d in dsts])
        g.remote_dma_fused([tr], local_sem=sem.sent)
        sent += NENG

    blk = list(range(KB * r, KB * r + KB))
    g.tensor.wait_ge(sem.b_in, 16)
    for n, i in enumerate(send_order(r) + [r]):
        senders = set(holder(i, k) for k in blk) - {rank}
        if senders:
            g.tensor.wait_ge(sem["A%d" % i], NENG * len(senders))
        if len(senders) < len(set(holder(i, k) for k in blk)):
            g.tensor.wait_ge(sem.a_in, 16)
        for t, k in enumerate(blk):
            if holder(i, k) == rank:
                lhsT = T.abuf[:, (k % KA) * M:(k % KA + 1) * M]
            else:
                lhsT = T.arecv[:, (i * KB + t) * M:(i * KB + t + 1) * M]
            mm = g.tensor.matmul(T["ps%d" % n][:], lhsT, T.bbuf[:, t * F:(t + 1) * F], start=(t == 0), stop=(t == KB - 1))
        mm.then_inc(sem["mm%d" % n], 1)

    for n, i in enumerate(send_order(r)):
        g.vector.wait_ge(sem["mm%d" % n], 1)
        g.vector.tensor_copy(T.pbuf[:, n * F:(n + 1) * F], T["ps%d" % n][:]).then_inc(sem["cp%d" % n], 1)
        dst = cores[i * GC + j]
        assert topo.may_write(core, dst)
        rid, pid, _ = topo.addr(dst)
        g.wait_ge(sem["cp%d" % n], 1)
        g.remote_dma(T.precv[:, n * F:(n + 1) * F], T.pbuf[:, n * F:(n + 1) * F], sem["P%d" % n], sem.sent,
                     pid, rid, pick(topo.mask(core, dst), NENG))
        sent += NENG
    g.wait_ge(sem.sent, sent)

    g.vector.wait_ge(sem.mm3, 1)
    acc = [T.ps3, T.acc0, T.acc1]
    for n in range(3):
        g.vector.wait_ge(sem["P%d" % n], NENG)
        if n > 0:
            g.vector.wait_ge(sem["ad%d" % (n - 1)], 1)
        out = T.ybuf[:] if n == 2 else acc[n + 1][:]
        g.vector.tensor_tensor(out, acc[n][:], T.precv[:, n * F:(n + 1) * F], AluOpType.add).then_inc(
            sem.y_done if n == 2 else sem["ad%d" % n], 1)
    g.sync.wait_ge(sem.y_done, 1)
    g.sync.dma_start(T.y[:], T.ybuf[:]).then_inc(sem.stored, 16)
    g.sync.wait_ge(sem.stored, 16)
